import numpy as np, ml_dtypes
CORES = [1,2,5,7,57,58,61,63,73,74,77,79]
N = 12
import mx_ref
NC = 128
def at(b): return (b, 0) if b < N else (2 * N - 1 - b, 1)
BF = ml_dtypes.bfloat16
def setup_inputs(rng):
    def f(*shape):
        return mx_ref.flush((rng.standard_normal(shape, dtype=np.float32) * np.exp2(rng.integers(-2, 3, shape[:-1] + (1,)))).astype(BF))
    return {"k": f(N, 128, 2 * 512), "q": f(N, 128, 2 * 4 * NC)}
def setup_inputs_blocks(rng):
    d = setup_inputs(rng)
    for k in ("k", "q"): d[k] = mx_ref.spread(d[k], rng, 4)
    return d
def setup_inputs_wide(rng):
    d = setup_inputs(rng)
    for k in ("k", "q"): d[k] = mx_ref.flush((d[k].astype(np.float32) * np.exp2(rng.integers(-8, 9, (N, 1, 1))).astype(np.float32)).astype(BF))
    return d
def setup_inputs_zeros(rng):
    d = setup_inputs(rng); v = d["q"].reshape(N, 128, -1, 4).copy()
    v[np.broadcast_to((rng.random((N, 1, v.shape[2], 1)) < 0.33), v.shape)] = 0
    d["q"] = v.reshape(d["q"].shape)
    return d
def reference(k, q):
    QK = [mx_ref.quantize(k[at(b)[0]][:, 512 * at(b)[1]:512 * at(b)[1] + 512]) for b in range(2 * N)]
    QQ = [mx_ref.quantize(q[at(b)[0]][:, 4 * NC * at(b)[1]:4 * NC * at(b)[1] + 4 * NC]) for b in range(2 * N)]
    y = np.zeros((N, 128, (2 * N + 1) * NC), np.float32)
    for r in range(N):
        c = 0
        for a in (r, 2 * N - 1 - r):
            for b in range(a + 1):
                y[r][:, c:c + NC] = mx_ref.matmul(QK[b], QQ[a]); c += NC
    return {"y": y}

@@ -1,0 +1,223 @@
+import comms_topo
+from concourse.bass import DstId, RemoteDMATransfer
+from concourse.mybir import dt, ActivationFunctionType
+
+CORES = [1, 2, 5, 7, 57, 58, 61, 63, 73, 74, 77, 79]
+N = 12
+W = 128
+BANKS = 8
+RUN = 4
+
+
+def build_plan(cores, topo):
+    n = len(cores)
+    chip = [topo.chip(c) for c in cores]
+    die = [topo.die(c) for c in cores]
+    chips = []
+    for ch in chip:
+        if ch not in chips:
+            chips.append(ch)
+    on = {ch: [r for r in range(n) if chip[r] == ch] for ch in chips}
+
+    def free(r):
+        return all(topo.may_write(cores[r], cores[x]) for x in range(n) if x != r)
+
+    keys = []
+    for r in range(n):
+        if (chip[r], die[r]) not in keys:
+            keys.append((chip[r], die[r]))
+    duo, base, slot = {}, {}, {}
+    for m, key in enumerate(keys):
+        rs = [r for r in on[key[0]] if die[r] == key[1]]
+        o = [r for r in rs if free(r)][-1]
+        e = [r for r in rs if r != o][0]
+        duo[key], base[key] = (e, o), 4 * m
+        slot[(e, 1)], slot[(e, 0)], slot[(o, 0)], slot[(o, 1)] = 4 * m, 4 * m + 1, 4 * m + 2, 4 * m + 3
+
+    def direct(X, Y):
+        return all(topo.may_write(cores[a], cores[b]) for a in on[X] for b in on[Y])
+
+    def wants1(X, Y):
+        return min(on[X]) > max(on[Y])
+
+    def sources(Y):
+        return sorted([X for X in chips if X != Y], key=lambda X: (not direct(X, Y), chips.index(X)))
+
+    def landing(Y, d, X):
+        return duo[(Y, d)][sources(Y).index(X) % 2]
+
+    def rng(X, d, Y):
+        b = base[(X, d)]
+        return (b, b + 4) if wants1(X, Y) else (b + 1, b + 3)
+
+    def masks(r):
+        here = [x for x in on[chip[r]] if x != r][0]
+        away = [x for x in range(n) if chip[x] != chip[r]][0]
+        full, out = topo.mask(cores[r], cores[here]), topo.mask(cores[r], cores[away])
+        return full, out, full & ~out
+
+    steps = {r: [] for r in range(n)}
+
+    def step(r, lo, hi, near, far, narrow):
+        full, out, stay = masks(r)
+        tr = []
+        if far:
+            tr.append((list(far), lo, hi, out))
+        if near:
+            tr.append((list(near), lo, hi, stay if (far or narrow) else full))
+        if tr:
+            steps[r].append(tr)
+
+    for key in keys:
+        X, d = key
+        e, o = duo[key]
+        for s in (e, o):
+            pair = (base[key], base[key] + 2) if s == e else (base[key] + 2, base[key] + 4)
+            t0 = (slot[(s, 0)], slot[(s, 0)] + 1)
+            lower = [x for x in on[X] if x < s]
+            higher = [x for x in on[X] if x > s]
+            relay = [Y for Y in chips if Y != X and not direct(X, Y)]
+            if s == e and relay:
+                both = o < s or any(wants1(X, Y) for Y in relay)
+                step(s, *(pair if both else t0), [o], [], False)
+                lower = [x for x in lower if x != o]
+                higher = [x for x in higher if x != o]
+            near_chips = [Y for Y in chips if Y != X and direct(X, Y)]
+            step(s, *pair, lower, [landing(Y, d, X) for Y in near_chips if wants1(X, Y)], s == o)
+            step(s, *t0, higher, [landing(Y, d, X) for Y in near_chips if not wants1(X, Y)], s == o)
+            if s == o:
+                by = {}
+                for Y in relay:
+                    by.setdefault(rng(X, d, Y), []).append(landing(Y, d, X))
+                for (lo, hi), far in sorted(by.items(), key=lambda kv: kv[0][0] - kv[0][1]):
+                    step(s, lo, hi, [], far, True)
+    for Y in chips:
+        for X in sources(Y):
+            for key in keys:
+                if key[0] == X:
+                    l = landing(Y, key[1], X)
+                    step(l, *rng(X, key[1], Y), [x for x in on[Y] if x != l], [], False)
+
+    lands = {r: [] for r in range(n)}
+    for r in range(n):
+        for tr in steps[r]:
+            for dsts, lo, hi, mask in tr:
+                for x in dsts:
+                    lands[x].append((lo, hi, 2 * bin(mask).count("1")))
+    groups = {r: [on[chip[r]]] + [on[X] for X in sources(chip[r])] for r in range(n)}
+    return {"slot": slot, "steps": steps, "lands": lands, "groups": groups}
+
+
+PLAN = build_plan(CORES, comms_topo)
+
+SCRATCH = {
+    "KB": ("sbuf", [128, 1024], "bfloat16"),
+    "QB": ("sbuf", [128, 1024], "bfloat16"),
+    "KC": ("sbuf", [128, 2 * N * W], "float8_e4m3fn_x4"),
+    "KS": ("sbuf", [128, 2 * N * W], "uint8"),
+    "QC": ("sbuf", [128, 2 * W], "float8_e4m3fn_x4"),
+    "QS": ("sbuf", [128, 2 * W], "uint8"),
+    "YB": ("sbuf", [128, (2 * N + 1) * W], "float32"),
+    "PS": ("psum", [128, 512 * BANKS], "float32"),
+}
+SEMAPHORES = (["ldk", "ldq", "kq", "qq", "sent", "st"]
+              + ["mm%d" % b for b in range(BANKS)] + ["ev%d" % b for b in range(BANKS)]
+              + sorted({"a%d_%d" % (lo, hi) for r in PLAN["lands"] for lo, hi, _ in PLAN["lands"][r]}))
+
+
+def rank_program(g, core, T, topo):
+    rank = T.rank_of(core)
+    if rank is None:
+        return
+    cores = list(T.cores)
+    slot, steps, lands = PLAN["slot"], PLAN["steps"][rank], PLAN["lands"][rank]
+    own = {slot[(rank, 0)], slot[(rank, 1)]}
+
+    def dep(sl):
+        if sl in own:
+            return ("kq", 2)
+        for lo, hi, cnt in lands:
+            if lo <= sl < hi:
+                return ("a%d_%d" % (lo, hi), cnt)
+        return None
+
+    g.sync.dma_start(T.KB[:], T.k[:]).then_inc(T.sem.ldk, 16)
+    g.sync.dma_start(T.QB[:], T.q[:]).then_inc(T.sem.ldq, 16)
+
+    g.vector.wait_ge(T.sem.ldk, 16)
+    for j in (0, 1):
+        a = slot[(rank, j)] * W
+        g.vector.quantize_mx(T.KC[:, a:a + W], T.KS[:, a:a + W], T.KB[:, 512 * j:512 * j + 512]).then_inc(T.sem.kq, 1)
+    g.vector.wait_ge(T.sem.ldq, 16)
+    g.vector.quantize_mx(T.QC[:], T.QS[:], T.QB[:]).then_inc(T.sem.qq, 1)
+
+    seen, sent = set(), 0
+    for tr in steps:
+        for _, lo, hi, _ in tr:
+            for sl in range(lo, hi):
+                d = dep(sl)
+                if d[0] not in seen:
+                    seen.add(d[0])
+                    g.wait_ge(T.sem[d[0]], d[1])
+        for codes in (True, False):
+            xs = []
+            for dsts, lo, hi, mask in tr:
+                def view():
+                    if codes:
+                        return T.KC[:, lo * W:hi * W].bitcast(dt.uint8)
+                    return T.KS[:, lo * W:hi * W]
+                ids = [DstId(rid=topo.addr(cores[x])[0], pnc=topo.addr(cores[x])[1]) for x in dsts]
+                xs.append(RemoteDMATransfer(dst_ids=ids, dma_engine_mask=mask, remote_sem=T.sem["a%d_%d" % (lo, hi)],
+                                            srcs=[view()], dsts=[view() for _ in dsts]))
+                sent += bin(mask).count("1")
+            g.remote_dma_fused(xs, local_sem=T.sem.sent)
+    if sent:
+        g.wait_ge(T.sem.sent, sent)
+
+    g.tensor.wait_ge(T.sem.kq, 2)
+    g.tensor.wait_ge(T.sem.qq, 1)
+    tseen, i, stores = {"kq"}, 0, 0
+    for grp in PLAN["groups"][rank]:
+        blocks = []
+        for s in grp:
+            if s <= rank:
+                blocks.append((s, slot[(s, 0)], 0))
+            blocks.append((rank + 1 + s, slot[(s, 0)], 1))
+            if s >= rank:
+                blocks.append((rank + 1 + 2 * N - 1 - s, slot[(s, 1)], 1))
+        blocks.sort()
+        runs = []
+        for blk in blocks:
+            if runs and runs[-1][-1][0] + 1 == blk[0] and len(runs[-1]) < RUN:
+                runs[-1].append(blk)
+            else:
+                runs.append([blk])
+        for run in runs:
+            need = {}
+            for idx, sl, qi in run:
+                d = dep(sl)
+                if d[0] not in tseen:
+                    tseen.add(d[0])
+                    g.tensor.wait_ge(T.sem[d[0]], d[1])
+                bank, use = i % BANKS, i // BANKS
+                if use:
+                    g.tensor.wait_ge(T.sem["ev%d" % bank], use)
+                ps = T.PS[:, 512 * bank:512 * bank + W]
+                g.tensor.matmul_mx(ps, T.KC[:, sl * W:sl * W + W], T.KS[:, sl * W:sl * W + W],
+                                   T.QC[:, qi * W:qi * W + W], T.QS[:, qi * W:qi * W + W],
+                                   True, True).then_inc(T.sem["mm%d" % bank], 1)
+                out = T.YB[:, idx * W:idx * W + W]
+                if bank % 2 == 0:
+                    g.vector.wait_ge(T.sem["mm%d" % bank], use + 1)
+                    g.vector.tensor_copy(out, ps).then_inc(T.sem["ev%d" % bank], 1)
+                else:
+                    g.scalar.wait_ge(T.sem["mm%d" % bank], use + 1)
+                    g.scalar.activation(out, ps, ActivationFunctionType.Copy).then_inc(T.sem["ev%d" % bank], 1)
+                need[bank] = use + 1
+                i += 1
+            for bank in sorted(need):
+                g.sync.wait_ge(T.sem["ev%d" % bank], need[bank])
+            a, b = run[0][0] * W, (run[-1][0] + 1) * W
+            g.sync.dma_start(T.y[:, a:b], T.YB[:, a:b]).then_inc(T.sem.st, 16)
+            stores += 1
+    g.sync.wait_ge(T.sem.st, 16 * stores)

@@ -66,7 +66,7 @@ def build_plan(cores, topo):
         if near:
             tr.append((list(near), lo, hi, stay if (far or narrow) else full))
         if tr:
-            steps[r].append(tr)
+            steps[r].append(("all", tr))
 
     for key in keys:
         X, d = key
@@ -83,28 +83,42 @@ def build_plan(cores, topo):
                 lower = [x for x in lower if x != o]
                 higher = [x for x in higher if x != o]
             near_chips = [Y for Y in chips if Y != X and direct(X, Y)]
-            step(s, *pair, lower, [landing(Y, d, X) for Y in near_chips if wants1(X, Y)], s == o)
-            step(s, *t0, higher, [landing(Y, d, X) for Y in near_chips if not wants1(X, Y)], s == o)
+            narrow = s == o and len(near_chips) > 0
+            step(s, *pair, lower, [landing(Y, d, X) for Y in near_chips if wants1(X, Y)], narrow)
+            step(s, *t0, higher, [landing(Y, d, X) for Y in near_chips if not wants1(X, Y)], narrow)
             if s == o:
                 by = {}
                 for Y in relay:
                     by.setdefault(rng(X, d, Y), []).append(landing(Y, d, X))
                 for (lo, hi), far in sorted(by.items(), key=lambda kv: kv[0][0] - kv[0][1]):
                     step(s, lo, hi, [], far, True)
+    items = {r: [] for r in range(n)}
     for Y in chips:
         for X in sources(Y):
             for key in keys:
                 if key[0] == X:
                     l = landing(Y, key[1], X)
-                    step(l, *rng(X, key[1], Y), [x for x in on[Y] if x != l], [], False)
+                    lo, hi = rng(X, key[1], Y)
+                    li, m = on[Y].index(l), len(on[Y])
+                    turn = [on[Y][(li + k) % m] for k in range(1, m)]
+                    steps[l].append(("turn", [(turn, lo, hi, masks(l)[0])]))
+                    h = 1 if direct(X, Y) else 2
+                    items[l].append((h, 0, lo, hi))
+                    for k, x in enumerate(turn):
+                        items[x].append((h + 1, k + 1, lo, hi))
 
     lands = {r: [] for r in range(n)}
     for r in range(n):
-        for tr in steps[r]:
+        for _, tr in steps[r]:
             for dsts, lo, hi, mask in tr:
                 for x in dsts:
-                    lands[x].append((lo, hi, 2 * bin(mask).count("1")))
-    groups = {r: [on[chip[r]]] + [on[X] for X in sources(chip[r])] for r in range(n)}
+                    lands[x].append((lo, hi, bin(mask).count("1")))
+    inv = {v: k for k, v in slot.items()}
+    groups = {}
+    for r in range(n):
+        groups[r] = [[(s, j) for s in on[chip[r]] for j in (0, 1)]]
+        for _, _, lo, hi in sorted(items[r]):
+            groups[r].append([inv[sl] for sl in range(lo, hi)])
     return {"slot": slot, "steps": steps, "lands": lands, "groups": groups}
 
 
@@ -122,7 +136,7 @@ SCRATCH = {
 }
 SEMAPHORES = (["ldk", "ldq", "kq", "qq", "sent", "st"]
               + ["mm%d" % b for b in range(BANKS)] + ["ev%d" % b for b in range(BANKS)]
-              + sorted({"a%d_%d" % (lo, hi) for r in PLAN["lands"] for lo, hi, _ in PLAN["lands"][r]}))
+              + sorted({"%s%d_%d" % (p, lo, hi) for p in "cs" for r in PLAN["lands"] for lo, hi, _ in PLAN["lands"][r]}))
 
 
 def rank_program(g, core, T, topo):
@@ -133,12 +147,12 @@ def rank_program(g, core, T, topo):
     slot, steps, lands = PLAN["slot"], PLAN["steps"][rank], PLAN["lands"][rank]
     own = {slot[(rank, 0)], slot[(rank, 1)]}
 
-    def dep(sl):
+    def dep(sl, p):
         if sl in own:
             return ("kq", 2)
         for lo, hi, cnt in lands:
             if lo <= sl < hi:
-                return ("a%d_%d" % (lo, hi), cnt)
+                return ("%s%d_%d" % (p, lo, hi), cnt)
         return None
 
     g.sync.dma_start(T.KB[:], T.k[:]).then_inc(T.sem.ldk, 16)
@@ -151,39 +165,49 @@ def rank_program(g, core, T, topo):
     g.vector.wait_ge(T.sem.ldq, 16)
     g.vector.quantize_mx(T.QC[:], T.QS[:], T.QB[:]).then_inc(T.sem.qq, 1)
 
-    seen, sent = set(), 0
-    for tr in steps:
-        for _, lo, hi, _ in tr:
+    sent, seen = [0], set()
+
+    def call(p, tr):
+        xs = []
+        for dsts, lo, hi, mask in tr:
             for sl in range(lo, hi):
-                d = dep(sl)
+                d = dep(sl, p)
                 if d[0] not in seen:
                     seen.add(d[0])
                     g.wait_ge(T.sem[d[0]], d[1])
-        for codes in (True, False):
-            xs = []
+
+            def view():
+                if p == "c":
+                    return T.KC[:, lo * W:hi * W].bitcast(dt.uint8)
+                return T.KS[:, lo * W:hi * W]
+            ids = [DstId(rid=topo.addr(cores[x])[0], pnc=topo.addr(cores[x])[1]) for x in dsts]
+            xs.append(RemoteDMATransfer(dst_ids=ids, dma_engine_mask=mask, remote_sem=T.sem["%s%d_%d" % (p, lo, hi)],
+                                        srcs=[view()], dsts=[view() for _ in dsts]))
+            sent[0] += bin(mask).count("1")
+        g.remote_dma_fused(xs, local_sem=T.sem.sent)
+
+    for kind, tr in steps:
+        call("s", tr)
+        if kind == "all":
+            call("c", tr)
+        else:
             for dsts, lo, hi, mask in tr:
-                def view():
-                    if codes:
-                        return T.KC[:, lo * W:hi * W].bitcast(dt.uint8)
-                    return T.KS[:, lo * W:hi * W]
-                ids = [DstId(rid=topo.addr(cores[x])[0], pnc=topo.addr(cores[x])[1]) for x in dsts]
-                xs.append(RemoteDMATransfer(dst_ids=ids, dma_engine_mask=mask, remote_sem=T.sem["a%d_%d" % (lo, hi)],
-                                            srcs=[view()], dsts=[view() for _ in dsts]))
-                sent += bin(mask).count("1")
-            g.remote_dma_fused(xs, local_sem=T.sem.sent)
-    if sent:
-        g.wait_ge(T.sem.sent, sent)
+                for x in dsts:
+                    call("c", [([x], lo, hi, mask)])
+    if sent[0]:
+        g.wait_ge(T.sem.sent, sent[0])
 
     g.tensor.wait_ge(T.sem.kq, 2)
     g.tensor.wait_ge(T.sem.qq, 1)
     tseen, i, stores = {"kq"}, 0, 0
     for grp in PLAN["groups"][rank]:
         blocks = []
-        for s in grp:
-            if s <= rank:
-                blocks.append((s, slot[(s, 0)], 0))
-            blocks.append((rank + 1 + s, slot[(s, 0)], 1))
-            if s >= rank:
+        for s, j in grp:
+            if j == 0:
+                if s <= rank:
+                    blocks.append((s, slot[(s, 0)], 0))
+                blocks.append((rank + 1 + s, slot[(s, 0)], 1))
+            elif s >= rank:
                 blocks.append((rank + 1 + 2 * N - 1 - s, slot[(s, 1)], 1))
         blocks.sort()
         runs = []
@@ -195,10 +219,11 @@ def rank_program(g, core, T, topo):
         for run in runs:
             need = {}
             for idx, sl, qi in run:
-                d = dep(sl)
-                if d[0] not in tseen:
-                    tseen.add(d[0])
-                    g.tensor.wait_ge(T.sem[d[0]], d[1])
+                for p in "sc":
+                    d = dep(sl, p)
+                    if d[0] not in tseen:
+                        tseen.add(d[0])
+                        g.tensor.wait_ge(T.sem[d[0]], d[1])
                 bank, use = i % BANKS, i // BANKS
                 if use:
                     g.tensor.wait_ge(T.sem["ev%d" % bank], use)

@@ -4,121 +4,137 @@ from concourse.mybir import dt, ActivationFunctionType
 
 CORES = [1, 2, 5, 7, 57, 58, 61, 63, 73, 74, 77, 79]
 N = 12
+NSIM = 80
 W = 128
 BANKS = 8
 RUN = 4
 
 
 def build_plan(cores, topo):
-    n = len(cores)
-    chip = [topo.chip(c) for c in cores]
-    die = [topo.die(c) for c in cores]
+    rk = {c: r for r, c in enumerate(cores)}
     chips = []
-    for ch in chip:
-        if ch not in chips:
-            chips.append(ch)
-    on = {ch: [r for r in range(n) if chip[r] == ch] for ch in chips}
+    for c in cores:
+        if topo.chip(c) not in chips:
+            chips.append(topo.chip(c))
+    on = {ch: [c for c in cores if topo.chip(c) == ch] for ch in chips}
 
-    def free(r):
-        return all(topo.may_write(cores[r], cores[x]) for x in range(n) if x != r)
+    def free(c):
+        return all(topo.may_write(c, x) for x in cores if x != c)
 
     keys = []
-    for r in range(n):
-        if (chip[r], die[r]) not in keys:
-            keys.append((chip[r], die[r]))
-    duo, base, slot = {}, {}, {}
+    for c in cores:
+        if (topo.chip(c), topo.die(c)) not in keys:
+            keys.append((topo.chip(c), topo.die(c)))
+    duo, aides, slot = {}, {}, {}
     for m, key in enumerate(keys):
-        rs = [r for r in on[key[0]] if die[r] == key[1]]
-        o = [r for r in rs if free(r)][-1]
-        e = [r for r in rs if r != o][0]
-        duo[key], base[key] = (e, o), 4 * m
-        slot[(e, 1)], slot[(e, 0)], slot[(o, 0)], slot[(o, 1)] = 4 * m, 4 * m + 1, 4 * m + 2, 4 * m + 3
+        rs = [c for c in on[key[0]] if topo.die(c) == key[1]]
+        o = [c for c in rs if free(c)][-1]
+        e = [c for c in rs if c != o][0]
+        duo[key] = (e, o)
+        slot[(rk[e], 1)], slot[(rk[e], 0)], slot[(rk[o], 0)], slot[(rk[o], 1)] = 4 * m, 4 * m + 1, 4 * m + 2, 4 * m + 3
+        spare = [c for c in range(NSIM) if (topo.chip(c), topo.die(c)) == key and c not in rk]
+        gate = [c for c in spare if free(c)][0]
+        aides[key] = ([c for c in spare if c != gate][0], gate)
+
+    def reach(c, Y):
+        return all(topo.may_write(c, x) for x in on[Y])
 
     def direct(X, Y):
-        return all(topo.may_write(cores[a], cores[b]) for a in on[X] for b in on[Y])
+        return all(reach(a, Y) for a in on[X])
 
     def wants1(X, Y):
-        return min(on[X]) > max(on[Y])
+        return min(rk[c] for c in on[X]) > max(rk[c] for c in on[Y])
 
-    def sources(Y):
-        return sorted([X for X in chips if X != Y], key=lambda X: (not direct(X, Y), chips.index(X)))
+    def pair(c):
+        a = min(slot[(rk[c], 0)], slot[(rk[c], 1)])
+        return (a, a + 2)
 
-    def landing(Y, d, X):
-        return duo[(Y, d)][sources(Y).index(X) % 2]
+    def t0(c):
+        return (slot[(rk[c], 0)], slot[(rk[c], 0)] + 1)
 
-    def rng(X, d, Y):
-        b = base[(X, d)]
-        return (b, b + 4) if wants1(X, Y) else (b + 1, b + 3)
+    def piece(c, Y):
+        return pair(c) if wants1(topo.chip(c), Y) else t0(c)
 
-    def masks(r):
-        here = [x for x in on[chip[r]] if x != r][0]
-        away = [x for x in range(n) if chip[x] != chip[r]][0]
-        full, out = topo.mask(cores[r], cores[here]), topo.mask(cores[r], cores[away])
+    land = {}
+    for Y, d in keys:
+        ps = []
+        for X in chips:
+            if X != Y and (X, d) in duo:
+                for s in duo[(X, d)]:
+                    lo, hi = piece(s, Y)
+                    ps.append((reach(s, Y), hi - lo, lo, s))
+        seats = list(duo[(Y, d)]) + list(aides[(Y, d)])
+        for i, p in enumerate(sorted(ps)):
+            land[(p[3], Y)] = seats[i % len(seats)]
+
+    def masks(c):
+        here = [x for x in on[topo.chip(c)] if x != c][0]
+        away = [x for x in cores if topo.chip(x) != topo.chip(c)][0]
+        full, out = topo.mask(c, here), topo.mask(c, away)
         return full, out, full & ~out
 
-    steps = {r: [] for r in range(n)}
+    steps = {}
 
-    def step(r, lo, hi, near, far, narrow):
-        full, out, stay = masks(r)
+    def step(c, lo, hi, near, far, narrow):
+        full, out, stay = masks(c)
         tr = []
         if far:
             tr.append((list(far), lo, hi, out))
         if near:
             tr.append((list(near), lo, hi, stay if (far or narrow) else full))
         if tr:
-            steps[r].append(("all", tr))
+            steps.setdefault(c, []).append(("all", tr))
+
+    def abroad(c, s, Ys):
+        by = {}
+        for Y in Ys:
+            by.setdefault(piece(s, Y), []).append(land[(s, Y)])
+        for (lo, hi), far in sorted(by.items(), key=lambda kv: kv[0][0] - kv[0][1]):
+            step(c, lo, hi, [], far, True)
 
     for key in keys:
-        X, d = key
-        e, o = duo[key]
-        for s in (e, o):
-            pair = (base[key], base[key] + 2) if s == e else (base[key] + 2, base[key] + 4)
-            t0 = (slot[(s, 0)], slot[(s, 0)] + 1)
-            lower = [x for x in on[X] if x < s]
-            higher = [x for x in on[X] if x > s]
-            relay = [Y for Y in chips if Y != X and not direct(X, Y)]
-            if s == e and relay:
-                both = o < s or any(wants1(X, Y) for Y in relay)
-                step(s, *(pair if both else t0), [o], [], False)
-                lower = [x for x in lower if x != o]
-                higher = [x for x in higher if x != o]
-            near_chips = [Y for Y in chips if Y != X and direct(X, Y)]
-            narrow = s == o and len(near_chips) > 0
-            step(s, *pair, lower, [landing(Y, d, X) for Y in near_chips if wants1(X, Y)], narrow)
-            step(s, *t0, higher, [landing(Y, d, X) for Y in near_chips if not wants1(X, Y)], narrow)
-            if s == o:
-                by = {}
-                for Y in relay:
-                    by.setdefault(rng(X, d, Y), []).append(landing(Y, d, X))
-                for (lo, hi), far in sorted(by.items(), key=lambda kv: kv[0][0] - kv[0][1]):
-                    step(s, lo, hi, [], far, True)
-    items = {r: [] for r in range(n)}
-    for Y in chips:
-        for X in sources(Y):
-            for key in keys:
-                if key[0] == X:
-                    l = landing(Y, key[1], X)
-                    lo, hi = rng(X, key[1], Y)
-                    li, m = on[Y].index(l), len(on[Y])
-                    turn = [on[Y][(li + k) % m] for k in range(1, m)]
-                    steps[l].append(("turn", [(turn, lo, hi, masks(l)[0])]))
-                    h = 1 if direct(X, Y) else 2
-                    items[l].append((h, 0, lo, hi))
-                    for k, x in enumerate(turn):
-                        items[x].append((h + 1, k + 1, lo, hi))
+        X = key[0]
+        gate = aides[key][1]
+        for s in duo[key]:
+            others = [Y for Y in chips if Y != X]
+            shut = [Y for Y in others if not reach(s, Y)]
+            if shut:
+                step(s, *(pair(s) if any(wants1(X, Y) for Y in shut) else t0(s)), [gate], [], False)
+                abroad(gate, s, shut)
+            abroad(s, s, [Y for Y in others if reach(s, Y) and not direct(X, Y)])
+            rest = [Y for Y in others if direct(X, Y)]
+            narrow = s == duo[key][1]
+            step(s, *pair(s), [x for x in on[X] if rk[x] < rk[s]], [land[(s, Y)] for Y in rest if wants1(X, Y)], narrow)
+            step(s, *t0(s), [x for x in on[X] if rk[x] > rk[s]], [land[(s, Y)] for Y in rest if not wants1(X, Y)], narrow)
 
-    lands = {r: [] for r in range(n)}
-    for r in range(n):
-        for _, tr in steps[r]:
+    items = {c: [] for c in cores}
+    for Y in chips:
+        arr = sorted((1 if reach(s, Y) else 2, piece(s, Y), l) for (s, Z), l in land.items() if Z == Y)
+        m, idle = len(on[Y]), 0
+        for h, (lo, hi), l in arr:
+            if l in rk:
+                li = on[Y].index(l)
+                turn = [on[Y][(li + k) % m] for k in range(1, m)]
+                items[l].append((h, 0, lo, hi))
+            else:
+                turn = [on[Y][(idle + k) % m] for k in range(m)]
+                idle += 1
+            steps.setdefault(l, []).append(("turn", [(turn, lo, hi, masks(l)[0])]))
+            for k, x in enumerate(turn):
+                items[x].append((h + 1, k + 1, lo, hi))
+
+    lands = {}
+    for c in steps:
+        for _, tr in steps[c]:
             for dsts, lo, hi, mask in tr:
                 for x in dsts:
-                    lands[x].append((lo, hi, bin(mask).count("1")))
+                    lands.setdefault(x, []).append((lo, hi, bin(mask).count("1")))
     inv = {v: k for k, v in slot.items()}
     groups = {}
-    for r in range(n):
-        groups[r] = [[(s, j) for s in on[chip[r]] for j in (0, 1)]]
-        for _, _, lo, hi in sorted(items[r]):
-            groups[r].append([inv[sl] for sl in range(lo, hi)])
+    for c in cores:
+        groups[c] = [[(rk[s], j) for s in on[topo.chip(c)] for j in (0, 1)]]
+        for _, _, lo, hi in sorted(items[c]):
+            groups[c].append([inv[sl] for sl in range(lo, hi)])
     return {"slot": slot, "steps": steps, "lands": lands, "groups": groups}
 
 
@@ -136,16 +152,16 @@ SCRATCH = {
 }
 SEMAPHORES = (["ldk", "ldq", "kq", "qq", "sent", "st"]
               + ["mm%d" % b for b in range(BANKS)] + ["ev%d" % b for b in range(BANKS)]
-              + sorted({"%s%d_%d" % (p, lo, hi) for p in "cs" for r in PLAN["lands"] for lo, hi, _ in PLAN["lands"][r]}))
+              + sorted({"%s%d_%d" % (p, lo, hi) for p in "cs" for c in PLAN["lands"] for lo, hi, _ in PLAN["lands"][c]}))
 
 
 def rank_program(g, core, T, topo):
     rank = T.rank_of(core)
-    if rank is None:
+    steps, lands = PLAN["steps"].get(core, []), PLAN["lands"].get(core, [])
+    if rank is None and not steps:
         return
-    cores = list(T.cores)
-    slot, steps, lands = PLAN["slot"], PLAN["steps"][rank], PLAN["lands"][rank]
-    own = {slot[(rank, 0)], slot[(rank, 1)]}
+    slot = PLAN["slot"]
+    own = set() if rank is None else {slot[(rank, 0)], slot[(rank, 1)]}
 
     def dep(sl, p):
         if sl in own:
@@ -155,15 +171,17 @@ def rank_program(g, core, T, topo):
                 return ("%s%d_%d" % (p, lo, hi), cnt)
         return None
 
-    g.sync.dma_start(T.KB[:], T.k[:]).then_inc(T.sem.ldk, 16)
-    g.sync.dma_start(T.QB[:], T.q[:]).then_inc(T.sem.ldq, 16)
+    if rank is not None:
+        g.sync.dma_start(T.KB[:], T.k[:]).then_inc(T.sem.ldk, 16)
+        g.sync.dma_start(T.QB[:], T.q[:]).then_inc(T.sem.ldq, 16)
 
-    g.vector.wait_ge(T.sem.ldk, 16)
-    for j in (0, 1):
-        a = slot[(rank, j)] * W
-        g.vector.quantize_mx(T.KC[:, a:a + W], T.KS[:, a:a + W], T.KB[:, 512 * j:512 * j + 512]).then_inc(T.sem.kq, 1)
-    g.vector.wait_ge(T.sem.ldq, 16)
-    g.vector.quantize_mx(T.QC[:], T.QS[:], T.QB[:]).then_inc(T.sem.qq, 1)
+        g.vector.wait_ge(T.sem.ldk, 16)
+        for j in (0, 1):
+            a = slot[(rank, j)] * W
+            g.vector.quantize_mx(T.KC[:, a:a + W], T.KS[:, a:a + W],
+                                 T.KB[:, 512 * j:512 * j + 512]).then_inc(T.sem.kq, 1)
+        g.vector.wait_ge(T.sem.ldq, 16)
+        g.vector.quantize_mx(T.QC[:], T.QS[:], T.QB[:]).then_inc(T.sem.qq, 1)
 
     sent, seen = [0], set()
 
@@ -180,7 +198,7 @@ def rank_program(g, core, T, topo):
                 if p == "c":
                     return T.KC[:, lo * W:hi * W].bitcast(dt.uint8)
                 return T.KS[:, lo * W:hi * W]
-            ids = [DstId(rid=topo.addr(cores[x])[0], pnc=topo.addr(cores[x])[1]) for x in dsts]
+            ids = [DstId(rid=topo.addr(x)[0], pnc=topo.addr(x)[1]) for x in dsts]
             xs.append(RemoteDMATransfer(dst_ids=ids, dma_engine_mask=mask, remote_sem=T.sem["%s%d_%d" % (p, lo, hi)],
                                         srcs=[view()], dsts=[view() for _ in dsts]))
             sent[0] += bin(mask).count("1")
@@ -196,11 +214,13 @@ def rank_program(g, core, T, topo):
                     call("c", [([x], lo, hi, mask)])
     if sent[0]:
         g.wait_ge(T.sem.sent, sent[0])
+    if rank is None:
+        return
 
     g.tensor.wait_ge(T.sem.kq, 2)
     g.tensor.wait_ge(T.sem.qq, 1)
     tseen, i, stores = {"kq"}, 0, 0
-    for grp in PLAN["groups"][rank]:
+    for grp in PLAN["groups"][core]:
         blocks = []
         for s, j in grp:
             if j == 0:

import comms_topo
from concourse.bass import DstId, RemoteDMATransfer
from concourse.mybir import dt, ActivationFunctionType

CORES = [1, 2, 5, 7, 57, 58, 61, 63, 73, 74, 77, 79]
N = 12
NSIM = 80
W = 128
BANKS = 8
RUN = 4


def build_plan(cores, topo):
    rk = {c: r for r, c in enumerate(cores)}
    chips = []
    for c in cores:
        if topo.chip(c) not in chips:
            chips.append(topo.chip(c))
    on = {ch: [c for c in cores if topo.chip(c) == ch] for ch in chips}

    def free(c):
        return all(topo.may_write(c, x) for x in cores if x != c)

    keys = []
    for c in cores:
        if (topo.chip(c), topo.die(c)) not in keys:
            keys.append((topo.chip(c), topo.die(c)))
    duo, aides, slot = {}, {}, {}
    for m, key in enumerate(keys):
        rs = [c for c in on[key[0]] if topo.die(c) == key[1]]
        o = [c for c in rs if free(c)][-1]
        e = [c for c in rs if c != o][0]
        duo[key] = (e, o)
        slot[(rk[e], 1)], slot[(rk[e], 0)], slot[(rk[o], 0)], slot[(rk[o], 1)] = 4 * m, 4 * m + 1, 4 * m + 2, 4 * m + 3
        spare = [c for c in range(NSIM) if (topo.chip(c), topo.die(c)) == key and c not in rk]
        gate = [c for c in spare if free(c)][0]
        aides[key] = ([c for c in spare if c != gate][0], gate)

    def reach(c, Y):
        return all(topo.may_write(c, x) for x in on[Y])

    def direct(X, Y):
        return all(reach(a, Y) for a in on[X])

    def wants1(X, Y):
        return min(rk[c] for c in on[X]) > max(rk[c] for c in on[Y])

    def pair(c):
        a = min(slot[(rk[c], 0)], slot[(rk[c], 1)])
        return (a, a + 2)

    def t0(c):
        return (slot[(rk[c], 0)], slot[(rk[c], 0)] + 1)

    def piece(c, Y):
        return pair(c) if wants1(topo.chip(c), Y) else t0(c)

    land = {}
    for Y, d in keys:
        ps = []
        for X in chips:
            if X != Y and (X, d) in duo:
                for s in duo[(X, d)]:
                    lo, hi = piece(s, Y)
                    ps.append((reach(s, Y), hi - lo, lo, s))
        seats = list(duo[(Y, d)]) + list(aides[(Y, d)])
        for i, p in enumerate(sorted(ps)):
            land[(p[3], Y)] = seats[i % len(seats)]

    def masks(c):
        here = [x for x in on[topo.chip(c)] if x != c][0]
        away = [x for x in cores if topo.chip(x) != topo.chip(c)][0]
        full, out = topo.mask(c, here), topo.mask(c, away)
        return full, out, full & ~out

    steps = {}

    def step(c, lo, hi, near, far, narrow):
        full, out, stay = masks(c)
        tr = []
        if far:
            tr.append((list(far), lo, hi, out))
        if near:
            tr.append((list(near), lo, hi, stay if (far or narrow) else full))
        if tr:
            steps.setdefault(c, []).append(("all", tr))

    def abroad(c, s, Ys):
        by = {}
        for Y in Ys:
            by.setdefault(piece(s, Y), []).append(land[(s, Y)])
        for (lo, hi), far in sorted(by.items(), key=lambda kv: kv[0][0] - kv[0][1]):
            step(c, lo, hi, [], far, True)

    for key in keys:
        X = key[0]
        gate = aides[key][1]
        for s in duo[key]:
            others = [Y for Y in chips if Y != X]
            shut = [Y for Y in others if not reach(s, Y)]
            if shut:
                step(s, *(pair(s) if any(wants1(X, Y) for Y in shut) else t0(s)), [gate], [], False)
                abroad(gate, s, shut)
            abroad(s, s, [Y for Y in others if reach(s, Y) and not direct(X, Y)])
            rest = [Y for Y in others if direct(X, Y)]
            narrow = s == duo[key][1]
            step(s, *pair(s), [x for x in on[X] if rk[x] < rk[s]], [land[(s, Y)] for Y in rest if wants1(X, Y)], narrow)
            step(s, *t0(s), [x for x in on[X] if rk[x] > rk[s]], [land[(s, Y)] for Y in rest if not wants1(X, Y)], narrow)

    items = {c: [] for c in cores}
    for Y in chips:
        arr = sorted((1 if reach(s, Y) else 2, piece(s, Y), l) for (s, Z), l in land.items() if Z == Y)
        m, idle = len(on[Y]), 0
        for h, (lo, hi), l in arr:
            if l in rk:
                li = on[Y].index(l)
                turn = [on[Y][(li + k) % m] for k in range(1, m)]
                items[l].append((h, 0, lo, hi))
            else:
                turn = [on[Y][(idle + k) % m] for k in range(m)]
                idle += 1
            steps.setdefault(l, []).append(("turn", [(turn, lo, hi, masks(l)[0])]))
            for k, x in enumerate(turn):
                items[x].append((h + 1, k + 1, lo, hi))

    lands = {}
    for c in steps:
        for _, tr in steps[c]:
            for dsts, lo, hi, mask in tr:
                for x in dsts:
                    lands.setdefault(x, []).append((lo, hi, bin(mask).count("1")))
    inv = {v: k for k, v in slot.items()}
    groups = {}
    for c in cores:
        groups[c] = [[(rk[s], j) for s in on[topo.chip(c)] for j in (0, 1)]]
        for _, _, lo, hi in sorted(items[c]):
            groups[c].append([inv[sl] for sl in range(lo, hi)])
    return {"slot": slot, "steps": steps, "lands": lands, "groups": groups}


PLAN = build_plan(CORES, comms_topo)

SCRATCH = {
    "KB": ("sbuf", [128, 1024], "bfloat16"),
    "QB": ("sbuf", [128, 1024], "bfloat16"),
    "KC": ("sbuf", [128, 2 * N * W], "float8_e4m3fn_x4"),
    "KS": ("sbuf", [128, 2 * N * W], "uint8"),
    "QC": ("sbuf", [128, 2 * W], "float8_e4m3fn_x4"),
    "QS": ("sbuf", [128, 2 * W], "uint8"),
    "YB": ("sbuf", [128, (2 * N + 1) * W], "float32"),
    "PS": ("psum", [128, 512 * BANKS], "float32"),
}
SEMAPHORES = (["ldk", "ldq", "kq", "qq", "sent", "st"]
              + ["mm%d" % b for b in range(BANKS)] + ["ev%d" % b for b in range(BANKS)]
              + sorted({"%s%d_%d" % (p, lo, hi) for p in "cs" for c in PLAN["lands"] for lo, hi, _ in PLAN["lands"][c]}))


def rank_program(g, core, T, topo):
    rank = T.rank_of(core)
    steps, lands = PLAN["steps"].get(core, []), PLAN["lands"].get(core, [])
    if rank is None and not steps:
        return
    slot = PLAN["slot"]
    own = set() if rank is None else {slot[(rank, 0)], slot[(rank, 1)]}

    def dep(sl, p):
        if sl in own:
            return ("kq", 2)
        for lo, hi, cnt in lands:
            if lo <= sl < hi:
                return ("%s%d_%d" % (p, lo, hi), cnt)
        return None

    if rank is not None:
        g.sync.dma_start(T.KB[:], T.k[:]).then_inc(T.sem.ldk, 16)
        g.sync.dma_start(T.QB[:], T.q[:]).then_inc(T.sem.ldq, 16)

        g.vector.wait_ge(T.sem.ldk, 16)
        for j in (0, 1):
            a = slot[(rank, j)] * W
            g.vector.quantize_mx(T.KC[:, a:a + W], T.KS[:, a:a + W],
                                 T.KB[:, 512 * j:512 * j + 512]).then_inc(T.sem.kq, 1)
        g.vector.wait_ge(T.sem.ldq, 16)
        g.vector.quantize_mx(T.QC[:], T.QS[:], T.QB[:]).then_inc(T.sem.qq, 1)

    sent, seen = [0], set()

    def call(p, tr):
        xs = []
        for dsts, lo, hi, mask in tr:
            for sl in range(lo, hi):
                d = dep(sl, p)
                if d[0] not in seen:
                    seen.add(d[0])
                    g.wait_ge(T.sem[d[0]], d[1])

            def view():
                if p == "c":
                    return T.KC[:, lo * W:hi * W].bitcast(dt.uint8)
                return T.KS[:, lo * W:hi * W]
            ids = [DstId(rid=topo.addr(x)[0], pnc=topo.addr(x)[1]) for x in dsts]
            xs.append(RemoteDMATransfer(dst_ids=ids, dma_engine_mask=mask, remote_sem=T.sem["%s%d_%d" % (p, lo, hi)],
                                        srcs=[view()], dsts=[view() for _ in dsts]))
            sent[0] += bin(mask).count("1")
        g.remote_dma_fused(xs, local_sem=T.sem.sent)

    for kind, tr in steps:
        call("s", tr)
        if kind == "all":
            call("c", tr)
        else:
            for dsts, lo, hi, mask in tr:
                for x in dsts:
                    call("c", [([x], lo, hi, mask)])
    if sent[0]:
        g.wait_ge(T.sem.sent, sent[0])
    if rank is None:
        return

    g.tensor.wait_ge(T.sem.kq, 2)
    g.tensor.wait_ge(T.sem.qq, 1)
    tseen, i, stores = {"kq"}, 0, 0
    for grp in PLAN["groups"][core]:
        blocks = []
        for s, j in grp:
            if j == 0:
                if s <= rank:
                    blocks.append((s, slot[(s, 0)], 0))
                blocks.append((rank + 1 + s, slot[(s, 0)], 1))
            elif s >= rank:
                blocks.append((rank + 1 + 2 * N - 1 - s, slot[(s, 1)], 1))
        blocks.sort()
        runs = []
        for blk in blocks:
            if runs and runs[-1][-1][0] + 1 == blk[0] and len(runs[-1]) < RUN:
                runs[-1].append(blk)
            else:
                runs.append([blk])
        for run in runs:
            need = {}
            for idx, sl, qi in run:
                for p in "sc":
                    d = dep(sl, p)
                    if d[0] not in tseen:
                        tseen.add(d[0])
                        g.tensor.wait_ge(T.sem[d[0]], d[1])
                bank, use = i % BANKS, i // BANKS
                if use:
                    g.tensor.wait_ge(T.sem["ev%d" % bank], use)
                ps = T.PS[:, 512 * bank:512 * bank + W]
                g.tensor.matmul_mx(ps, T.KC[:, sl * W:sl * W + W], T.KS[:, sl * W:sl * W + W],
                                   T.QC[:, qi * W:qi * W + W], T.QS[:, qi * W:qi * W + W],
                                   True, True).then_inc(T.sem["mm%d" % bank], 1)
                out = T.YB[:, idx * W:idx * W + W]
                if bank % 2 == 0:
                    g.vector.wait_ge(T.sem["mm%d" % bank], use + 1)
                    g.vector.tensor_copy(out, ps).then_inc(T.sem["ev%d" % bank], 1)
                else:
                    g.scalar.wait_ge(T.sem["mm%d" % bank], use + 1)
                    g.scalar.activation(out, ps, ActivationFunctionType.Copy).then_inc(T.sem["ev%d" % bank], 1)
                need[bank] = use + 1
                i += 1
            for bank in sorted(need):
                g.sync.wait_ge(T.sem["ev%d" % bank], need[bank])
            a, b = run[0][0] * W, (run[-1][0] + 1) * W
            g.sync.dma_start(T.y[:, a:b], T.YB[:, a:b]).then_inc(T.sem.st, 16)
            stores += 1
    g.sync.wait_ge(T.sem.st, 16 * stores)
